import numpy as np
import ml_dtypes


def mxq(x, axis, fmt="e4m3"):
    dtype, down = {"e4m3": (ml_dtypes.float8_e4m3fn, 7), "e5m2": (ml_dtypes.float8_e5m2, 14)}[fmt]
    v = np.moveaxis(np.asarray(x, np.float32).astype(ml_dtypes.bfloat16).astype(np.float64), axis, -1)
    blocks = v.reshape(v.shape[:-1] + (-1, 32))
    amax = np.abs(blocks).max(-1, keepdims=True)
    byte = np.maximum(np.where(amax > 0, np.frexp(amax)[1] - 1 + 127, 0) - down, 1)
    scale = np.exp2(byte - 127.0)
    codes = (blocks / scale).astype(np.float32).astype(dtype).astype(np.float64)
    return np.moveaxis((codes * scale).reshape(v.shape), -1, axis)


WIDE = False


def mx_kscale(k):
    if not WIDE:
        return np.ones(k)
    levels = np.array([10, -10, 5, -5, 0])
    if k % 512:
        return np.exp2(np.random.permutation(np.resize(levels, k // 32))).repeat(32)
    a = np.empty((k // 512, 16))
    for p in range(k // 512):
        a[p, :8] = np.random.permutation(np.resize(levels, 8))
        for g in range(8):
            far = levels[np.abs(levels - a[p, g]) >= 10]
            a[p, g + 8] = far[np.random.randint(len(far))]
    return np.exp2(a.ravel()).repeat(32)


def f64(x):
    return np.asarray(x).astype(np.float64)


def striped(idx):
    return np.tile(np.asarray(idx).reshape(-1, 16).T, (8, 1)).astype(np.uint16)


def unstriped(offs):
    return offs[:16].T.reshape(-1).astype(np.int64)


E2M1 = np.array([0.0, 0.5, 1.0, 1.5, 2.0, 3.0, 4.0, 6.0, -0.0, -0.5, -1.0, -1.5, -2.0, -3.0, -4.0, -6.0])


def pack_weight(w, fmt):
    k, n = w.shape
    w = f64(np.asarray(w, np.float32).astype(ml_dtypes.bfloat16)).reshape(k // 32, 32, n)
    amax = np.abs(w).max(1)
    if fmt == "e4m3":
        byte = np.frexp(amax)[1] - 1 + 127 - 7
    else:
        mant, ex = np.frexp(amax / 6.0)
        byte = np.where(mant > 0.5, ex, ex - 1) + 127
    byte = np.clip(np.where(amax > 0, byte, 1), 1, 254)
    scaled = (w * np.exp2(127.0 - byte)[:, None, :]).reshape(k, n).astype(np.float32)
    by_word = np.ascontiguousarray(scaled.reshape(k // 512, 128, 4, n).transpose(0, 1, 3, 2))
    if fmt == "e4m3":
        words = by_word.astype(ml_dtypes.float8_e4m3fn).view(np.uint8)
    else:
        c = by_word.astype(ml_dtypes.float4_e2m1fn).view(np.uint8) & 0xF
        words = (c[..., 0::2] | (c[..., 1::2] << 4)).reshape(k // 512, 128, 2 * n)
    return np.ascontiguousarray(words), np.ascontiguousarray(byte.astype(np.uint8).reshape(k // 512, 16, n))


def unpack_weight(words, scales, fmt):
    g, _, n = scales.shape
    words = np.ascontiguousarray(words).reshape(g, 128, n, -1)
    if fmt == "e4m3":
        vals = words.view(ml_dtypes.float8_e4m3fn).astype(np.float64)
    else:
        nib = np.empty((g, 128, n, 4), np.uint8)
        nib[..., 0::2] = words & 0xF
        nib[..., 1::2] = words >> 4
        vals = E2M1[nib]
    vals = vals * np.repeat(np.exp2(scales.astype(np.float64) - 127.0), 8, axis=1)[..., None]
    return vals.transpose(0, 1, 3, 2).reshape(g * 512, n)


def bf(x):
    return np.asarray(x, np.float32).astype(ml_dtypes.bfloat16)


def planes(Y):
    r, m = Y.shape
    b = f64(bf(Y)).reshape(r // 32, 32, m)
    amax = np.abs(b).max(1)
    byte = np.clip(np.where(amax > 0, np.frexp(amax)[1] - 1 + 127 - 7, 1), 1, 254)
    codes = (b * np.exp2(127.0 - byte)[:, None, :]).reshape(r, m).astype(np.float32).astype(ml_dtypes.float8_e4m3fn).view(np.uint8)
    words = codes.reshape(r // 512, 128, 4, m).transpose(0, 1, 3, 2)
    return np.ascontiguousarray(words), np.ascontiguousarray(byte.astype(np.uint8).reshape(r // 512, 16, m))


K, L, T, J, N = 512, 512, 1024, 512, 512


def setup_inputs():
    n = np.random.standard_normal
    idx = np.random.permutation(T)[:J]
    fk = mx_kscale(K)
    fl = mx_kscale(L)
    xap = pack_weight(n((K, J)) / fk[:, None], "e4m3")
    xbp = pack_weight(n((L, J)) / fl[:, None], "e2m1")
    wbp = pack_weight(n((L, N)) * 1 / np.sqrt(L) * fl[:, None], "e4m3")
    return {
        "xa_words": xap[0],
        "xa_scales": xap[1],
        "wa": (n((K, N)) * 1 / np.sqrt(K) * fk[:, None]).astype(np.float32),
        "xb_words": xbp[0],
        "xb_scales": xbp[1],
        "wb_words": wbp[0],
        "wb_scales": wbp[1],
        "old": (1.0 * n((N, T))).astype(np.float32),
        "offs": striped(idx),
    }


def reference(xa_words, xa_scales, wa, xb_words, xb_scales, wb_words, wb_scales, old, offs):
    idx = unstriped(offs)
    xau = unpack_weight(xa_words, xa_scales, "e4m3")
    xbu = unpack_weight(xb_words, xb_scales, "e2m1")
    wbu = unpack_weight(wb_words, wb_scales, "e4m3")
    waq = mxq(f64(wa), 0, "e4m3")
    v = waq.T @ xau + wbu.T @ xbu
    fd = 0.9 * f64(old)
    d = np.maximum(v - fd[:, idx], 0.0)
    p = np.zeros((N, T))
    p[:, idx] = d
    y = fd + p
    words, scales = planes(y)
    return y, words, scales

@@ -1,0 +1,195 @@
+from contextlib import ExitStack
+
+import concourse.mybir as mybir
+
+K, T, J, N = 512, 1024, 512, 512
+P, PACK = 128, 4
+FADE = 0.9
+FLOPS = 2 * 2 * K * N * J
+
+F32 = mybir.dt.float32
+BF16 = mybir.dt.bfloat16
+I32 = mybir.dt.int32
+U16 = mybir.dt.uint16
+U8 = mybir.dt.uint8
+FP8X4 = mybir.dt.float8_e4m3fn_x4
+FP4X4 = mybir.dt.float4_e2m1fn_x4
+ALU = mybir.AluOpType
+ACT = mybir.ActivationFunctionType
+
+CHUNKS = 4
+CW = T // CHUNKS
+
+
+def tile_list_page_running_peak_pl_kernel(
+    tc, xa_words, xa_scales, wa, xb_words, xb_scales, wb_words, wb_scales, old, offs, out_0, out_1, out_2
+):
+    nc = tc.nc
+    with ExitStack() as ctx:
+        keep = ctx.enter_context(tc.tile_pool(name="keep", bufs=1))
+        psum = ctx.enter_context(tc.psum_pool(name="psum", bufs=1))
+
+        def tile(name, shape, dtype, tag=""):
+            return keep.tile(shape, dtype, name=name, tag=tag or name, align_bytes=64)
+
+        def load_scale_rows(queue, plane, scales, quadrants):
+            for q in quadrants:
+                queue.dma_start(
+                    out=plane[32 * q : 32 * q + 4, :].bitcast(I32),
+                    in_=scales[0, 4 * q : 4 * q + 4, :].bitcast(I32),
+                )
+
+        offsets = keep.tile([P, J // 16], U16, name="offsets")
+        old_rows = old.rearrange("(p t) c -> p t c", t=PACK)
+        out_rows = out_0.rearrange("(p t) c -> p t c", t=PACK)
+
+        old_sb = [tile(f"old{t}", [P, T], F32) for t in range(PACK)]
+        fd = [tile(f"fd{t}", [P, T], F32) for t in range(PACK)]
+        pages = [tile(f"page{t}", [P, T], F32) for t in range(PACK - 1)]
+        page = [pages[t % (PACK - 1)] for t in range(PACK)]
+        wa_raw = tile("wa_raw", [P, PACK, N], F32)
+        xa_c = tile("xa_c", [P, J], I32)
+        xb_c = tile("xb_c", [P, 2 * J], U8)
+        wb_raw = tile("wb_raw", [P, N], I32)
+        xa_s = tile("xa_s", [P, J], U8)
+        xb_s = tile("xb_s", [P, J], U8)
+        wb_s_raw = tile("wb_s_raw", [P, N], U8)
+
+        nc.gpsimd.memset(wb_s_raw[:].bitcast(I32), 0)
+        load_scale_rows(nc.gpsimd, xb_s, xb_scales, range(3))
+
+        nc.sync.dma_start(out=old_sb[0][:], in_=old_rows[:, 0, :])
+        load_scale_rows(nc.sync, xa_s, xa_scales, range(4))
+        nc.sync.dma_start(offsets[:], offs)
+        load_scale_rows(nc.sync, wb_s_raw, wb_scales, range(1))
+        nc.sync.dma_start(out=wa_raw[:], in_=wa.rearrange("(p j) n -> p j n", j=PACK))
+        load_scale_rows(nc.sync, wb_s_raw, wb_scales, range(1, 4))
+        load_scale_rows(nc.sync, xb_s, xb_scales, range(3, 4))
+        nc.sync.dma_start(out=wb_raw[:], in_=wb_words[0].rearrange("p n r -> p (n r)").bitcast(I32))
+        nc.sync.dma_start(out=xa_c[:], in_=xa_words[0].rearrange("p n r -> p (n r)").bitcast(I32))
+        nc.sync.dma_start(out=xb_c[:].bitcast(I32), in_=xb_words[0].bitcast(I32))
+        for t in range(1, PACK):
+            nc.sync.dma_start(out=old_sb[t][:], in_=old_rows[:, t, :])
+
+        for fresh in pages:
+            nc.vector.memset(fresh[:], 0.0)
+
+        picked = tile("picked", [P, J], F32)
+        neg_picked = tile("neg_picked", [P, J], F32)
+        nc.vector.tensor_scalar_mul(fd[0][:], old_sb[0][:], FADE)
+        nc.vector.tensor_copy(out=picked[:], in_=fd[0][:].indirect(offsets[:]))
+        nc.scalar.activation(out=neg_picked[:], in_=picked[:], func=ACT.Copy, scale=-1.0)
+
+        wa_first = tile("wa_first", [P, P, PACK], BF16)
+        wa_rest = tile("wa_rest", [P, PACK - 1, P, PACK], BF16)
+        wa_dealt = wa_raw[:].rearrange("p j (m t) -> p m t j", t=PACK)
+        wa_c = [tile(f"wa_c{t}", [P, P], I32) for t in range(2)]
+        wa_s = [tile(f"wa_s{t}", [P, P], U8) for t in range(2)]
+        wa_c23 = tile("wa_c23", [P, 2 * P], I32)
+        wa_s23 = tile("wa_s23", [P, 2 * P], U8)
+        wb_c = tile("wb_c", [P, N], I32)
+        wb_s = tile("wb_s", [P, N], U8)
+
+        nc.vector.tensor_copy(out=wa_first[:], in_=wa_dealt[:, :, 0, :])
+        nc.scalar.copy(out=wa_rest[:].rearrange("p t m j -> p m t j"), in_=wa_dealt[:, :, 1:, :])
+        nc.vector.tensor_copy(
+            out=wb_s[:].rearrange("p (t m) -> p m t", t=PACK), in_=wb_s_raw[:].rearrange("p (m t) -> p m t", t=PACK)
+        )
+        nc.vector.quantize_mx(
+            out=wa_c[0][:].bitcast(FP8X4), scales=wa_s[0][:], in_=wa_first[:].rearrange("p m j -> p (m j)")
+        )
+        nc.vector.tensor_copy(
+            out=wb_c[:].rearrange("p (t m) -> p m t", t=PACK), in_=wb_raw[:].rearrange("p (m t) -> p m t", t=PACK)
+        )
+
+        def product(t, codes, scales):
+            acc = psum.tile([P, J], F32, name=f"v{t}")
+            cols = slice(t * P, (t + 1) * P)
+            nc.tensor.matmul_mx(
+                out=acc[:], lhsT=codes.bitcast(FP8X4), lhsT_scale=scales,
+                rhs=xa_c[:].bitcast(FP8X4), rhs_scale=xa_s[:], start=True, stop=False,
+            )
+            nc.tensor.matmul_mx(
+                out=acc[:], lhsT=wb_c[:, cols].bitcast(FP8X4), lhsT_scale=wb_s[:, cols],
+                rhs=xb_c[:].bitcast(FP4X4), rhs_scale=xb_s[:], start=False, stop=True,
+            )
+            return acc
+
+        v = [product(0, wa_c[0][:], wa_s[0][:])]
+        nc.vector.quantize_mx(
+            out=wa_c[1][:].bitcast(FP8X4), scales=wa_s[1][:], in_=wa_rest[:, 0].rearrange("p m j -> p (m j)")
+        )
+        nc.vector.quantize_mx(
+            out=wa_c23[:].bitcast(FP8X4), scales=wa_s23[:], in_=wa_rest[:, 1:].rearrange("p t m j -> p (t m j)")
+        )
+        larger = tile("larger", [P, J], F32, tag="wa_rest")
+        nc.vector.tensor_tensor(out=larger[:], in0=v[0][:], in1=picked[:], op=ALU.max)
+        nc.vector.tensor_tensor(out=page[0][:].indirect(offsets[:]), in0=larger[:], in1=neg_picked[:], op=ALU.add)
+
+        v.append(product(1, wa_c[1][:], wa_s[1][:]))
+        v.append(product(2, wa_c23[:, :P], wa_s23[:, :P]))
+        v.append(product(3, wa_c23[:, P:], wa_s23[:, P:]))
+
+        v_sb = {t: tile(f"v_sb{t}", [P, J], F32) for t in range(1, PACK)}
+        gap = {t: tile(f"gap{t}", [P, J], F32) for t in range(1, PACK)}
+        yb = [tile(f"yb{c}", [P, CW, PACK], BF16) for c in range(CHUNKS)]
+        y_c = tile("y_c", [P, T], I32)
+        y_s = tile("y_s", [P, T], U8)
+
+        for t in range(1, PACK):
+            nc.scalar.copy(out=v_sb[t][:], in_=v[t][:])
+            nc.scalar.activation(out=fd[t][:], in_=old_sb[t][:], func=ACT.Copy, scale=FADE)
+        d = {t: tile(f"d{t}", [P, J], F32, tag=f"old{PACK - t}" if t > 1 else "old3") for t in range(1, PACK)}
+
+        def look_up(t):
+            nc.vector.tensor_tensor(out=gap[t][:], in0=fd[t][:].indirect(offsets[:]), in1=v_sb[t][:], op=ALU.subtract)
+            nc.scalar.activation(out=d[t][:], in_=gap[t][:], func=ACT.Relu, scale=-1.0)
+
+        def put(t):
+            nc.vector.tensor_copy(out=page[t][:].indirect(offsets[:]), in_=d[t][:])
+
+        def add_whole(t):
+            nc.gpsimd.tensor_tensor(out=y[t // 2][:, t % 2, :], in0=fd[t][:], in1=page[t][:], op=ALU.add)
+            nc.sync.dma_start(out=out_rows[:, t, :], in_=y[t // 2][:, t % 2, :])
+
+        def pair_view(h, c):
+            cols = slice(c * CW, (c + 1) * CW)
+            return yb[c][:, :, 2 * h : 2 * h + 2], y[h][:, :, cols].rearrange("p t c -> p c t")
+
+        for t in range(1, PACK):
+            look_up(t)
+        y = [tile("y0", [P, 2, T], F32, tag="v_sb3"), tile("y1", [P, 2, T], F32)]
+        add_whole(0)
+        put(1)
+        add_whole(1)
+        put(2)
+        for c in range(CHUNKS):
+            dst, src = pair_view(0, c)
+            nc.scalar.copy(out=dst, in_=src)
+        add_whole(2)
+        put(3)
+
+        words_out = out_1[0].rearrange("p c r -> p (c r)").bitcast(I32)
+        for c in range(CHUNKS):
+            cols = slice(c * CW, (c + 1) * CW)
+            nc.vector.tensor_tensor(out=y[1][:, 1, cols], in0=fd[3][:, cols], in1=page[3][:, cols], op=ALU.add)
+            if c % 2 == 1:
+                both = slice((c - 1) * CW, (c + 1) * CW)
+                nc.sync.dma_start(out=out_rows[:, 3, both], in_=y[1][:, 1, both])
+            dst, src = pair_view(1, c)
+            if c < CHUNKS - 1:
+                nc.scalar.copy(out=dst, in_=src)
+        dst, src = pair_view(1, CHUNKS - 1)
+        nc.vector.tensor_copy(out=dst, in_=src)
+        for c in (0, 3, 1, 2):
+            cols = slice(c * CW, (c + 1) * CW)
+            nc.vector.quantize_mx(
+                out=y_c[:, cols].bitcast(FP8X4), scales=y_s[:, cols], in_=yb[c][:].rearrange("p c t -> p (c t)")
+            )
+        for h in range(2):
+            both = slice(h * 2 * CW, (h + 1) * 2 * CW)
+            nc.sync.dma_start(out=words_out[:, both], in_=y_c[:, both])
+        for q in range(4):
+            nc.scalar.dma_start(
+                out=out_2[0, 4 * q : 4 * q + 4, :].bitcast(I32), in_=y_s[32 * q : 32 * q + 4, :].bitcast(I32)
+            )

@@ -45,8 +45,8 @@ def tile_list_page_running_peak_pl_kernel(
 
         old_sb = [tile(f"old{t}", [P, T], F32) for t in range(PACK)]
         fd = [tile(f"fd{t}", [P, T], F32) for t in range(PACK)]
-        pages = [tile(f"page{t}", [P, T], F32) for t in range(PACK - 1)]
-        page = [pages[t % (PACK - 1)] for t in range(PACK)]
+        pages = [tile(f"page{t}", [P, T], F32) for t in range(2)]
+        page = [pages[t % 2] for t in range(PACK)]
         wa_raw = tile("wa_raw", [P, PACK, N], F32)
         xa_c = tile("xa_c", [P, J], I32)
         xb_c = tile("xb_c", [P, 2 * J], U8)
@@ -56,79 +56,75 @@ def tile_list_page_running_peak_pl_kernel(
         wb_s_raw = tile("wb_s_raw", [P, N], U8)
 
         nc.gpsimd.memset(wb_s_raw[:].bitcast(I32), 0)
-        load_scale_rows(nc.gpsimd, xb_s, xb_scales, range(3))
+        load_scale_rows(nc.gpsimd, xa_s, xa_scales, range(1, 4))
 
         nc.sync.dma_start(out=old_sb[0][:], in_=old_rows[:, 0, :])
-        load_scale_rows(nc.sync, xa_s, xa_scales, range(4))
         nc.sync.dma_start(offsets[:], offs)
-        load_scale_rows(nc.sync, wb_s_raw, wb_scales, range(1))
-        nc.sync.dma_start(out=wa_raw[:], in_=wa.rearrange("(p j) n -> p j n", j=PACK))
-        load_scale_rows(nc.sync, wb_s_raw, wb_scales, range(1, 4))
-        load_scale_rows(nc.sync, xb_s, xb_scales, range(3, 4))
         nc.sync.dma_start(out=wb_raw[:], in_=wb_words[0].rearrange("p n r -> p (n r)").bitcast(I32))
-        nc.sync.dma_start(out=xa_c[:], in_=xa_words[0].rearrange("p n r -> p (n r)").bitcast(I32))
+        load_scale_rows(nc.sync, wb_s_raw, wb_scales, range(4))
+        nc.sync.dma_start(out=wa_raw[:], in_=wa.rearrange("(p j) n -> p j n", j=PACK))
+        load_scale_rows(nc.sync, xb_s, xb_scales, range(4))
         nc.sync.dma_start(out=xb_c[:].bitcast(I32), in_=xb_words[0].bitcast(I32))
+        nc.sync.dma_start(out=xa_c[:], in_=xa_words[0].rearrange("p n r -> p (n r)").bitcast(I32))
+        load_scale_rows(nc.sync, xa_s, xa_scales, range(1))
         for t in range(1, PACK):
             nc.sync.dma_start(out=old_sb[t][:], in_=old_rows[:, t, :])
 
-        for fresh in pages:
-            nc.vector.memset(fresh[:], 0.0)
+        nc.vector.memset(pages[0][:], 0.0)
+        nc.vector.memset(pages[1][:], 0.0)
 
-        picked = tile("picked", [P, J], F32)
+        picked = [tile(f"picked{t}", [P, J], F32) for t in range(PACK)]
         neg_picked = tile("neg_picked", [P, J], F32)
         nc.vector.tensor_scalar_mul(fd[0][:], old_sb[0][:], FADE)
-        nc.vector.tensor_copy(out=picked[:], in_=fd[0][:].indirect(offsets[:]))
-        nc.scalar.activation(out=neg_picked[:], in_=picked[:], func=ACT.Copy, scale=-1.0)
+        nc.vector.tensor_copy(out=picked[0][:], in_=fd[0][:].indirect(offsets[:]))
+        nc.scalar.activation(out=neg_picked[:], in_=picked[0][:], func=ACT.Copy, scale=-1.0)
 
-        wa_first = tile("wa_first", [P, P, PACK], BF16)
-        wa_rest = tile("wa_rest", [P, PACK - 1, P, PACK], BF16)
+        wa_bf = [tile(f"wa_bf{h}", [P, 2, P, PACK], BF16) for h in range(2)]
+        wa_c = [tile("wa_c0", [P, 2 * P], I32)]
+        wa_s = [tile(f"wa_s{h}", [P, 2 * P], U8) for h in range(2)]
         wa_dealt = wa_raw[:].rearrange("p j (m t) -> p m t j", t=PACK)
-        wa_c = [tile(f"wa_c{t}", [P, P], I32) for t in range(2)]
-        wa_s = [tile(f"wa_s{t}", [P, P], U8) for t in range(2)]
-        wa_c23 = tile("wa_c23", [P, 2 * P], I32)
-        wa_s23 = tile("wa_s23", [P, 2 * P], U8)
         wb_c = tile("wb_c", [P, N], I32)
         wb_s = tile("wb_s", [P, N], U8)
 
-        nc.vector.tensor_copy(out=wa_first[:], in_=wa_dealt[:, :, 0, :])
-        nc.scalar.copy(out=wa_rest[:].rearrange("p t m j -> p m t j"), in_=wa_dealt[:, :, 1:, :])
-        nc.vector.tensor_copy(
-            out=wb_s[:].rearrange("p (t m) -> p m t", t=PACK), in_=wb_s_raw[:].rearrange("p (m t) -> p m t", t=PACK)
-        )
-        nc.vector.quantize_mx(
-            out=wa_c[0][:].bitcast(FP8X4), scales=wa_s[0][:], in_=wa_first[:].rearrange("p m j -> p (m j)")
-        )
+        def quantise_wa(h):
+            nc.vector.quantize_mx(
+                out=wa_c[h][:].bitcast(FP8X4), scales=wa_s[h][:], in_=wa_bf[h][:].rearrange("p t m j -> p (t m j)")
+            )
+
         nc.vector.tensor_copy(
             out=wb_c[:].rearrange("p (t m) -> p m t", t=PACK), in_=wb_raw[:].rearrange("p (m t) -> p m t", t=PACK)
         )
+        nc.vector.tensor_copy(
+            out=wb_s[:].rearrange("p (t m) -> p m t", t=PACK), in_=wb_s_raw[:].rearrange("p (m t) -> p m t", t=PACK)
+        )
+        nc.vector.tensor_copy(out=wa_bf[0][:].rearrange("p t m j -> p m t j"), in_=wa_dealt[:, :, 0:2, :])
+        nc.scalar.copy(out=wa_bf[1][:].rearrange("p t m j -> p m t j"), in_=wa_dealt[:, :, 2:4, :])
+        quantise_wa(0)
 
-        def product(t, codes, scales):
+        def product(t):
             acc = psum.tile([P, J], F32, name=f"v{t}")
             cols = slice(t * P, (t + 1) * P)
-            nc.tensor.matmul_mx(
-                out=acc[:], lhsT=codes.bitcast(FP8X4), lhsT_scale=scales,
-                rhs=xa_c[:].bitcast(FP8X4), rhs_scale=xa_s[:], start=True, stop=False,
-            )
-            nc.tensor.matmul_mx(
-                out=acc[:], lhsT=wb_c[:, cols].bitcast(FP8X4), lhsT_scale=wb_s[:, cols],
-                rhs=xb_c[:].bitcast(FP4X4), rhs_scale=xb_s[:], start=False, stop=True,
-            )
+            half = slice(t % 2 * P, (t % 2 + 1) * P)
+            passes = [
+                (wa_c[t // 2][:, half], wa_s[t // 2][:, half], xa_c[:].bitcast(FP8X4), xa_s[:]),
+                (wb_c[:, cols], wb_s[:, cols], xb_c[:].bitcast(FP4X4), xb_s[:]),
+            ]
+            if t == 0:
+                passes = passes[::-1]
+            for i, (w, w_scale, x, x_scale) in enumerate(passes):
+                nc.tensor.matmul_mx(
+                    out=acc[:], lhsT=w.bitcast(FP8X4), lhsT_scale=w_scale, rhs=x, rhs_scale=x_scale,
+                    start=(i == 0), stop=(i == 1),
+                )
             return acc
 
-        v = [product(0, wa_c[0][:], wa_s[0][:])]
-        nc.vector.quantize_mx(
-            out=wa_c[1][:].bitcast(FP8X4), scales=wa_s[1][:], in_=wa_rest[:, 0].rearrange("p m j -> p (m j)")
-        )
-        nc.vector.quantize_mx(
-            out=wa_c23[:].bitcast(FP8X4), scales=wa_s23[:], in_=wa_rest[:, 1:].rearrange("p t m j -> p (t m j)")
-        )
-        larger = tile("larger", [P, J], F32, tag="wa_rest")
-        nc.vector.tensor_tensor(out=larger[:], in0=v[0][:], in1=picked[:], op=ALU.max)
+        v = [product(t) for t in range(2)]
+        larger = tile("larger", [P, J], F32)
+        nc.vector.tensor_tensor(out=larger[:], in0=v[0][:], in1=picked[0][:], op=ALU.max)
+        wa_c.append(tile("wa_c1", [P, 2 * P], I32, tag="picked0"))
+        quantise_wa(1)
+        v.extend(product(t) for t in range(2, PACK))
         nc.vector.tensor_tensor(out=page[0][:].indirect(offsets[:]), in0=larger[:], in1=neg_picked[:], op=ALU.add)
-
-        v.append(product(1, wa_c[1][:], wa_s[1][:]))
-        v.append(product(2, wa_c23[:, :P], wa_s23[:, :P]))
-        v.append(product(3, wa_c23[:, P:], wa_s23[:, P:]))
 
         v_sb = {t: tile(f"v_sb{t}", [P, J], F32) for t in range(1, PACK)}
         gap = {t: tile(f"gap{t}", [P, J], F32) for t in range(1, PACK)}
@@ -137,29 +133,34 @@ def tile_list_page_running_peak_pl_kernel(
         y_s = tile("y_s", [P, T], U8)
 
         for t in range(1, PACK):
-            nc.scalar.copy(out=v_sb[t][:], in_=v[t][:])
             nc.scalar.activation(out=fd[t][:], in_=old_sb[t][:], func=ACT.Copy, scale=FADE)
-        d = {t: tile(f"d{t}", [P, J], F32, tag=f"old{PACK - t}" if t > 1 else "old3") for t in range(1, PACK)}
+            nc.scalar.copy(out=v_sb[t][:], in_=v[t][:])
+        d = {t: tile(f"d{t}", [P, J], F32, tag=f"old{PACK - t}") for t in range(1, PACK)}
 
         def look_up(t):
-            nc.vector.tensor_tensor(out=gap[t][:], in0=fd[t][:].indirect(offsets[:]), in1=v_sb[t][:], op=ALU.subtract)
-            nc.scalar.activation(out=d[t][:], in_=gap[t][:], func=ACT.Relu, scale=-1.0)
+            nc.vector.tensor_copy(out=picked[t][:], in_=fd[t][:].indirect(offsets[:]))
+            nc.gpsimd.tensor_tensor(out=gap[t][:], in0=v_sb[t][:], in1=picked[t][:], op=ALU.subtract)
+            nc.scalar.activation(out=d[t][:], in_=gap[t][:], func=ACT.Relu)
 
         def put(t):
             nc.vector.tensor_copy(out=page[t][:].indirect(offsets[:]), in_=d[t][:])
 
+        def chunked(rows):
+            return rows.rearrange("p (c w) -> p c w", w=CW)
+
         def add_whole(t):
-            nc.gpsimd.tensor_tensor(out=y[t // 2][:, t % 2, :], in0=fd[t][:], in1=page[t][:], op=ALU.add)
-            nc.sync.dma_start(out=out_rows[:, t, :], in_=y[t // 2][:, t % 2, :])
+            rows = y[t // 2][:, :, t % 2, :]
+            nc.gpsimd.tensor_tensor(out=rows, in0=chunked(fd[t][:]), in1=chunked(page[t][:]), op=ALU.add)
+            nc.sync.dma_start(out=chunked(out_rows[:, t, :]), in_=rows)
 
         def pair_view(h, c):
-            cols = slice(c * CW, (c + 1) * CW)
-            return yb[c][:, :, 2 * h : 2 * h + 2], y[h][:, :, cols].rearrange("p t c -> p c t")
+            return yb[c][:, :, 2 * h : 2 * h + 2], y[h][:, c].rearrange("p t w -> p w t")
 
-        for t in range(1, PACK):
-            look_up(t)
-        y = [tile("y0", [P, 2, T], F32, tag="v_sb3"), tile("y1", [P, 2, T], F32)]
+        look_up(1)
+        look_up(2)
+        y = [tile("y0", [P, CHUNKS, 2, CW], F32, tag="v_sb2"), tile("y1", [P, CHUNKS, 2, CW], F32)]
         add_whole(0)
+        look_up(3)
         put(1)
         add_whole(1)
         put(2)
@@ -172,10 +173,10 @@ def tile_list_page_running_peak_pl_kernel(
         words_out = out_1[0].rearrange("p c r -> p (c r)").bitcast(I32)
         for c in range(CHUNKS):
             cols = slice(c * CW, (c + 1) * CW)
-            nc.vector.tensor_tensor(out=y[1][:, 1, cols], in0=fd[3][:, cols], in1=page[3][:, cols], op=ALU.add)
+            nc.vector.tensor_tensor(out=y[1][:, c, 1, :], in0=fd[3][:, cols], in1=page[3][:, cols], op=ALU.add)
             if c % 2 == 1:
-                both = slice((c - 1) * CW, (c + 1) * CW)
-                nc.sync.dma_start(out=out_rows[:, 3, both], in_=y[1][:, 1, both])
+                both = slice(c - 1, c + 1)
+                nc.sync.dma_start(out=chunked(out_rows[:, 3, :])[:, both, :], in_=y[1][:, both, 1, :])
             dst, src = pair_view(1, c)
             if c < CHUNKS - 1:
                 nc.scalar.copy(out=dst, in_=src)
@@ -186,10 +187,8 @@ def tile_list_page_running_peak_pl_kernel(
             nc.vector.quantize_mx(
                 out=y_c[:, cols].bitcast(FP8X4), scales=y_s[:, cols], in_=yb[c][:].rearrange("p c t -> p (c t)")
             )
-        for h in range(2):
-            both = slice(h * 2 * CW, (h + 1) * 2 * CW)
-            nc.sync.dma_start(out=words_out[:, both], in_=y_c[:, both])
+            nc.sync.dma_start(out=words_out[:, cols], in_=y_c[:, cols])
         for q in range(4):
-            nc.scalar.dma_start(
+            (nc.sync if q < 2 else nc.scalar).dma_start(
                 out=out_2[0, 4 * q : 4 * q + 4, :].bitcast(I32), in_=y_s[32 * q : 32 * q + 4, :].bitcast(I32)
             )

@@ -73,14 +73,14 @@ def tile_list_page_running_peak_pl_kernel(
         nc.vector.memset(pages[0][:], 0.0)
         nc.vector.memset(pages[1][:], 0.0)
 
-        picked = [tile(f"picked{t}", [P, J], F32) for t in range(PACK)]
+        picked = [tile("picked0", [P, J], F32)]
         neg_picked = tile("neg_picked", [P, J], F32)
         nc.vector.tensor_scalar_mul(fd[0][:], old_sb[0][:], FADE)
         nc.vector.tensor_copy(out=picked[0][:], in_=fd[0][:].indirect(offsets[:]))
         nc.scalar.activation(out=neg_picked[:], in_=picked[0][:], func=ACT.Copy, scale=-1.0)
 
         wa_bf = [tile(f"wa_bf{h}", [P, 2, P, PACK], BF16) for h in range(2)]
-        wa_c = [tile("wa_c0", [P, 2 * P], I32)]
+        wa_c = [tile(f"wa_c{h}", [P, 2 * P], I32) for h in range(2)]
         wa_s = [tile(f"wa_s{h}", [P, 2 * P], U8) for h in range(2)]
         wa_dealt = wa_raw[:].rearrange("p j (m t) -> p m t j", t=PACK)
         wb_c = tile("wb_c", [P, N], I32)
@@ -100,6 +100,7 @@ def tile_list_page_running_peak_pl_kernel(
         nc.vector.tensor_copy(out=wa_bf[0][:].rearrange("p t m j -> p m t j"), in_=wa_dealt[:, :, 0:2, :])
         nc.scalar.copy(out=wa_bf[1][:].rearrange("p t m j -> p m t j"), in_=wa_dealt[:, :, 2:4, :])
         quantise_wa(0)
+        quantise_wa(1)
 
         def product(t):
             acc = psum.tile([P, J], F32, name=f"v{t}")
@@ -118,12 +119,9 @@ def tile_list_page_running_peak_pl_kernel(
                 )
             return acc
 
-        v = [product(t) for t in range(2)]
+        v = [product(t) for t in range(PACK)]
         larger = tile("larger", [P, J], F32)
         nc.vector.tensor_tensor(out=larger[:], in0=v[0][:], in1=picked[0][:], op=ALU.max)
-        wa_c.append(tile("wa_c1", [P, 2 * P], I32, tag="picked0"))
-        quantise_wa(1)
-        v.extend(product(t) for t in range(2, PACK))
         nc.vector.tensor_tensor(out=page[0][:].indirect(offsets[:]), in0=larger[:], in1=neg_picked[:], op=ALU.add)
 
         v_sb = {t: tile(f"v_sb{t}", [P, J], F32) for t in range(1, PACK)}
@@ -138,9 +136,8 @@ def tile_list_page_running_peak_pl_kernel(
         d = {t: tile(f"d{t}", [P, J], F32, tag=f"old{PACK - t}") for t in range(1, PACK)}
 
         def look_up(t):
-            nc.vector.tensor_copy(out=picked[t][:], in_=fd[t][:].indirect(offsets[:]))
-            nc.gpsimd.tensor_tensor(out=gap[t][:], in0=v_sb[t][:], in1=picked[t][:], op=ALU.subtract)
-            nc.scalar.activation(out=d[t][:], in_=gap[t][:], func=ACT.Relu)
+            nc.vector.tensor_tensor(out=gap[t][:], in0=fd[t][:].indirect(offsets[:]), in1=v_sb[t][:], op=ALU.subtract)
+            nc.scalar.activation(out=d[t][:], in_=gap[t][:], func=ACT.Relu, scale=-1.0)
 
         def put(t):
             nc.vector.tensor_copy(out=page[t][:].indirect(offsets[:]), in_=d[t][:])
@@ -158,9 +155,9 @@ def tile_list_page_running_peak_pl_kernel(
 
         look_up(1)
         look_up(2)
-        y = [tile("y0", [P, CHUNKS, 2, CW], F32, tag="v_sb2"), tile("y1", [P, CHUNKS, 2, CW], F32)]
-        add_whole(0)
         look_up(3)
+        y = [tile("y0", [P, CHUNKS, 2, CW], F32, tag="v_sb3"), tile("y1", [P, CHUNKS, 2, CW], F32)]
+        add_whole(0)
         put(1)
         add_whole(1)
         put(2)

from contextlib import ExitStack

import concourse.mybir as mybir

K, T, J, N = 512, 1024, 512, 512
P, PACK = 128, 4
FADE = 0.9
FLOPS = 2 * 2 * K * N * J

F32 = mybir.dt.float32
BF16 = mybir.dt.bfloat16
I32 = mybir.dt.int32
U16 = mybir.dt.uint16
U8 = mybir.dt.uint8
FP8X4 = mybir.dt.float8_e4m3fn_x4
FP4X4 = mybir.dt.float4_e2m1fn_x4
ALU = mybir.AluOpType
ACT = mybir.ActivationFunctionType

CHUNKS = 4
CW = T // CHUNKS


def tile_list_page_running_peak_pl_kernel(
    tc, xa_words, xa_scales, wa, xb_words, xb_scales, wb_words, wb_scales, old, offs, out_0, out_1, out_2
):
    nc = tc.nc
    with ExitStack() as ctx:
        keep = ctx.enter_context(tc.tile_pool(name="keep", bufs=1))
        psum = ctx.enter_context(tc.psum_pool(name="psum", bufs=1))

        def tile(name, shape, dtype, tag=""):
            return keep.tile(shape, dtype, name=name, tag=tag or name, align_bytes=64)

        def load_scale_rows(queue, plane, scales, quadrants):
            for q in quadrants:
                queue.dma_start(
                    out=plane[32 * q : 32 * q + 4, :].bitcast(I32),
                    in_=scales[0, 4 * q : 4 * q + 4, :].bitcast(I32),
                )

        offsets = keep.tile([P, J // 16], U16, name="offsets")
        old_rows = old.rearrange("(p t) c -> p t c", t=PACK)
        out_rows = out_0.rearrange("(p t) c -> p t c", t=PACK)

        old_sb = [tile(f"old{t}", [P, T], F32) for t in range(PACK)]
        fd = [tile(f"fd{t}", [P, T], F32) for t in range(PACK)]
        pages = [tile(f"page{t}", [P, T], F32) for t in range(2)]
        page = [pages[t % 2] for t in range(PACK)]
        wa_raw = tile("wa_raw", [P, PACK, N], F32)
        xa_c = tile("xa_c", [P, J], I32)
        xb_c = tile("xb_c", [P, 2 * J], U8)
        wb_raw = tile("wb_raw", [P, N], I32)
        xa_s = tile("xa_s", [P, J], U8)
        xb_s = tile("xb_s", [P, J], U8)
        wb_s_raw = tile("wb_s_raw", [P, N], U8)

        nc.gpsimd.memset(wb_s_raw[:].bitcast(I32), 0)
        load_scale_rows(nc.gpsimd, xa_s, xa_scales, range(1, 4))

        nc.sync.dma_start(out=old_sb[0][:], in_=old_rows[:, 0, :])
        nc.sync.dma_start(offsets[:], offs)
        nc.sync.dma_start(out=wb_raw[:], in_=wb_words[0].rearrange("p n r -> p (n r)").bitcast(I32))
        load_scale_rows(nc.sync, wb_s_raw, wb_scales, range(4))
        nc.sync.dma_start(out=wa_raw[:], in_=wa.rearrange("(p j) n -> p j n", j=PACK))
        load_scale_rows(nc.sync, xb_s, xb_scales, range(4))
        nc.sync.dma_start(out=xb_c[:].bitcast(I32), in_=xb_words[0].bitcast(I32))
        nc.sync.dma_start(out=xa_c[:], in_=xa_words[0].rearrange("p n r -> p (n r)").bitcast(I32))
        load_scale_rows(nc.sync, xa_s, xa_scales, range(1))
        for t in range(1, PACK):
            nc.sync.dma_start(out=old_sb[t][:], in_=old_rows[:, t, :])

        nc.vector.memset(pages[0][:], 0.0)
        nc.vector.memset(pages[1][:], 0.0)

        picked = [tile("picked0", [P, J], F32)]
        neg_picked = tile("neg_picked", [P, J], F32)
        nc.vector.tensor_scalar_mul(fd[0][:], old_sb[0][:], FADE)
        nc.vector.tensor_copy(out=picked[0][:], in_=fd[0][:].indirect(offsets[:]))
        nc.scalar.activation(out=neg_picked[:], in_=picked[0][:], func=ACT.Copy, scale=-1.0)

        wa_bf = [tile(f"wa_bf{h}", [P, 2, P, PACK], BF16) for h in range(2)]
        wa_c = [tile(f"wa_c{h}", [P, 2 * P], I32) for h in range(2)]
        wa_s = [tile(f"wa_s{h}", [P, 2 * P], U8) for h in range(2)]
        wa_dealt = wa_raw[:].rearrange("p j (m t) -> p m t j", t=PACK)
        wb_c = tile("wb_c", [P, N], I32)
        wb_s = tile("wb_s", [P, N], U8)

        def quantise_wa(h):
            nc.vector.quantize_mx(
                out=wa_c[h][:].bitcast(FP8X4), scales=wa_s[h][:], in_=wa_bf[h][:].rearrange("p t m j -> p (t m j)")
            )

        nc.vector.tensor_copy(
            out=wb_c[:].rearrange("p (t m) -> p m t", t=PACK), in_=wb_raw[:].rearrange("p (m t) -> p m t", t=PACK)
        )
        nc.vector.tensor_copy(
            out=wb_s[:].rearrange("p (t m) -> p m t", t=PACK), in_=wb_s_raw[:].rearrange("p (m t) -> p m t", t=PACK)
        )
        nc.vector.tensor_copy(out=wa_bf[0][:].rearrange("p t m j -> p m t j"), in_=wa_dealt[:, :, 0:2, :])
        nc.scalar.copy(out=wa_bf[1][:].rearrange("p t m j -> p m t j"), in_=wa_dealt[:, :, 2:4, :])
        quantise_wa(0)
        quantise_wa(1)

        def product(t):
            acc = psum.tile([P, J], F32, name=f"v{t}")
            cols = slice(t * P, (t + 1) * P)
            half = slice(t % 2 * P, (t % 2 + 1) * P)
            passes = [
                (wa_c[t // 2][:, half], wa_s[t // 2][:, half], xa_c[:].bitcast(FP8X4), xa_s[:]),
                (wb_c[:, cols], wb_s[:, cols], xb_c[:].bitcast(FP4X4), xb_s[:]),
            ]
            if t == 0:
                passes = passes[::-1]
            for i, (w, w_scale, x, x_scale) in enumerate(passes):
                nc.tensor.matmul_mx(
                    out=acc[:], lhsT=w.bitcast(FP8X4), lhsT_scale=w_scale, rhs=x, rhs_scale=x_scale,
                    start=(i == 0), stop=(i == 1),
                )
            return acc

        v = [product(t) for t in range(PACK)]
        larger = tile("larger", [P, J], F32)
        nc.vector.tensor_tensor(out=larger[:], in0=v[0][:], in1=picked[0][:], op=ALU.max)
        nc.vector.tensor_tensor(out=page[0][:].indirect(offsets[:]), in0=larger[:], in1=neg_picked[:], op=ALU.add)

        v_sb = {t: tile(f"v_sb{t}", [P, J], F32) for t in range(1, PACK)}
        gap = {t: tile(f"gap{t}", [P, J], F32) for t in range(1, PACK)}
        yb = [tile(f"yb{c}", [P, CW, PACK], BF16) for c in range(CHUNKS)]
        y_c = tile("y_c", [P, T], I32)
        y_s = tile("y_s", [P, T], U8)

        for t in range(1, PACK):
            nc.scalar.activation(out=fd[t][:], in_=old_sb[t][:], func=ACT.Copy, scale=FADE)
            nc.scalar.copy(out=v_sb[t][:], in_=v[t][:])
        d = {t: tile(f"d{t}", [P, J], F32, tag=f"old{PACK - t}") for t in range(1, PACK)}

        def look_up(t):
            nc.vector.tensor_tensor(out=gap[t][:], in0=fd[t][:].indirect(offsets[:]), in1=v_sb[t][:], op=ALU.subtract)
            nc.scalar.activation(out=d[t][:], in_=gap[t][:], func=ACT.Relu, scale=-1.0)

        def put(t):
            nc.vector.tensor_copy(out=page[t][:].indirect(offsets[:]), in_=d[t][:])

        def chunked(rows):
            return rows.rearrange("p (c w) -> p c w", w=CW)

        def add_whole(t):
            rows = y[t // 2][:, :, t % 2, :]
            nc.gpsimd.tensor_tensor(out=rows, in0=chunked(fd[t][:]), in1=chunked(page[t][:]), op=ALU.add)
            nc.sync.dma_start(out=chunked(out_rows[:, t, :]), in_=rows)

        def pair_view(h, c):
            return yb[c][:, :, 2 * h : 2 * h + 2], y[h][:, c].rearrange("p t w -> p w t")

        look_up(1)
        look_up(2)
        look_up(3)
        y = [tile("y0", [P, CHUNKS, 2, CW], F32, tag="v_sb3"), tile("y1", [P, CHUNKS, 2, CW], F32)]
        add_whole(0)
        put(1)
        add_whole(1)
        put(2)
        for c in range(CHUNKS):
            dst, src = pair_view(0, c)
            nc.scalar.copy(out=dst, in_=src)
        add_whole(2)
        put(3)

        words_out = out_1[0].rearrange("p c r -> p (c r)").bitcast(I32)
        for c in range(CHUNKS):
            cols = slice(c * CW, (c + 1) * CW)
            nc.vector.tensor_tensor(out=y[1][:, c, 1, :], in0=fd[3][:, cols], in1=page[3][:, cols], op=ALU.add)
            if c % 2 == 1:
                both = slice(c - 1, c + 1)
                nc.sync.dma_start(out=chunked(out_rows[:, 3, :])[:, both, :], in_=y[1][:, both, 1, :])
            dst, src = pair_view(1, c)
            if c < CHUNKS - 1:
                nc.scalar.copy(out=dst, in_=src)
        dst, src = pair_view(1, CHUNKS - 1)
        nc.vector.tensor_copy(out=dst, in_=src)
        for c in (0, 3, 1, 2):
            cols = slice(c * CW, (c + 1) * CW)
            nc.vector.quantize_mx(
                out=y_c[:, cols].bitcast(FP8X4), scales=y_s[:, cols], in_=yb[c][:].rearrange("p c t -> p (c t)")
            )
            nc.sync.dma_start(out=words_out[:, cols], in_=y_c[:, cols])
        for q in range(4):
            (nc.sync if q < 2 else nc.scalar).dma_start(
                out=out_2[0, 4 * q : 4 * q + 4, :].bitcast(I32), in_=y_s[32 * q : 32 * q + 4, :].bitcast(I32)
            )
